import numpy as np, ml_dtypes
CORES = [50,106,114,52,108,116]
N = 6
R, TK = 64, 128
def setup_inputs(rng):
    v = (rng.standard_normal((N, 128, R), dtype=np.float32) / np.float32(np.sqrt(128 * N))).astype(ml_dtypes.bfloat16)
    return {"x": rng.standard_normal((N, 128, TK), dtype=np.float32).astype(ml_dtypes.bfloat16), "v": v, "vt": v.transpose(0, 2, 1).copy()}
def setup_inputs_big(rng):
    d = setup_inputs(rng)
    for k in ("x",): d[k] = (d[k].astype(np.float32) * 1048576.0).astype(d[k].dtype)
    return d
def setup_inputs_small(rng):
    d = setup_inputs(rng)
    for k in ("x",): d[k] = (d[k].astype(np.float32) * (1 / 1048576.0)).astype(d[k].dtype)
    return d
def setup_inputs_apart(rng):
    d = setup_inputs(rng)
    f = (10.0 ** rng.permutation(np.linspace(-1.5, 1.5, N))).astype(np.float32).reshape(N, 1, 1)
    for k in ("x",): d[k] = (d[k].astype(np.float32) * f).astype(d[k].dtype)
    return d
def reference(x, v, vt):
    X, V, VT = x.astype(np.float64), v.astype(np.float64), vt.astype(np.float64)
    t = sum(V[j].T @ X[j] for j in range(N))
    return {"y": np.stack([X[r] - 2.0 * (VT[r].T @ t) for r in range(N)]).astype(ml_dtypes.bfloat16)}

from concourse.bass import DstId, RemoteDMATransfer
from concourse.mybir import AluOpType

H = 64
ENGINES = 8

SCRATCH = {
    "xs": ("sbuf", [128, 128], "bfloat16"),
    "vs": ("sbuf", [128, H], "bfloat16"),
    "vts": ("sbuf", [128, 128], "bfloat16"),
    "vt2": ("sbuf", [128, 128], "bfloat16"),
    "p": ("sbuf", [128, H], "bfloat16"),
    "nb": ("sbuf", [128, H], "bfloat16"),
    "cs0": ("sbuf", [128, H], "bfloat16"),
    "cs1": ("sbuf", [128, H], "bfloat16"),
    "cs2": ("sbuf", [128, H], "bfloat16"),
    "ys": ("sbuf", [128, 128], "bfloat16"),
    "pp": ("psum", [128, 512], "float32"),
    "ya": ("psum", [128, 512], "float32"),
    "yb": ("psum", [128, 512], "float32"),
}
SEMAPHORES = ["ld", "ldvt", "mm", "pc", "dbl", "nbs", "c0", "c1", "c2", "fa", "fb", "yv", "st", "loc"]


def lowest(mask, n):
    out, bit = 0, 1
    while n and bit <= mask:
        if mask & bit:
            out |= bit
            n -= 1
        bit <<= 1
    return out


def plan(cores, topo):
    chips = sorted({topo.chip(c) for c in cores})
    members = {ch: [c for c in cores if topo.chip(c) == ch] for ch in chips}
    jobs = []
    for a in chips:
        for b in chips:
            if a != b:
                jobs.append((a, b, [s for s in members[a] if all(topo.may_write(s, d) for d in members[b])]))
    jobs.sort(key=lambda j: len(j[2]))
    load = {c: 0 for c in cores}
    sends = {c: [] for c in cores}
    sender = {}
    for a, b, able in jobs:
        s = min(able, key=lambda c: load[c])
        load[s] += len(members[b])
        sends[s] += members[b]
        sender[(a, b)] = s
    return chips, members, sends, sender, load


def rank_program(g, core, T, topo):
    if T.rank_of(core) is None:
        return
    S = T.sem
    chips, members, sends, sender, load = plan(list(T.cores), topo)
    mine = topo.chip(core)
    (buddy,) = [c for c in members[mine] if c != core]
    far = sends[core]

    g.sync.dma_start(T.xs[:], T.x[:]).then_inc(S.ld, 16)
    g.scalar.dma_start(T.vs[:], T.v[:]).then_inc(S.ld, 16)
    g.sync.dma_start(T.vts[0:H, :], T.vt[:]).then_inc(S.ldvt, 16)
    g.scalar.dma_start(T.vts[H:128, :], T.vt[:]).then_inc(S.ldvt, 16)

    g.tensor.wait_ge(S.ld, 32)
    g.tensor.matmul(T.pp[0:H, 0:H], T.vs[:], T.xs[:, 0:H], start=True, stop=True).then_inc(S.mm, 1)
    g.tensor.matmul(T.pp[H:128, 0:H], T.vs[:], T.xs[:, H:128], start=True, stop=True).then_inc(S.mm, 1)
    g.vector.wait_ge(S.mm, 2)
    g.vector.tensor_copy(T.p[:], T.pp[:, 0:H]).then_inc(S.pc, 1)
    g.vector.wait_ge(S.ldvt, 32)
    g.vector.tensor_tensor(T.vt2[:], T.vts[:], T.vts[:], AluOpType.add).then_inc(S.dbl, 1)

    common = topo.mask(core, buddy)
    for d in far:
        common &= topo.mask(core, d)
    mask = lowest(common, ENGINES)
    sent = 0
    rid, pid, _ = topo.addr(buddy)
    g.wait_ge(S.pc, 1)
    g.remote_dma(T.nb[:], T.p[:], S.nbs, S.loc, pid, rid, mask)
    sent += ENGINES
    if far:
        k = chips.index(mine)
        ids = []
        for d in far:
            rid, pid, _ = topo.addr(d)
            ids.append(DstId(rid=rid, pnc=pid))
        g.wait_ge(S.nbs, ENGINES)
        g.remote_dma_fused([RemoteDMATransfer(dst_ids=ids, dma_engine_mask=mask, remote_sem=S["c%d" % k],
                                              srcs=[T.p[:], T.nb[:]], dsts=[T["cs%d" % k][:] for _ in far],
                                              alu_op=1)], local_sem=S.loc)
        sent += ENGINES

    others = sorted([ch for ch in chips if ch != mine], key=lambda ch: load[sender[(ch, mine)]])
    pieces = [(T.p, S.pc, 1), (T.nb, S.nbs, ENGINES)]
    pieces += [(T["cs%d" % chips.index(ch)], S["c%d" % chips.index(ch)], ENGINES) for ch in others]
    g.tensor.wait_ge(S.dbl, 1)
    for i, (buf, sem, n) in enumerate(pieces):
        first, last = i == 0, i == len(pieces) - 1
        g.tensor.wait_ge(sem, n)
        a = g.tensor.matmul(T.ya[:, 0:H], T.vt2[0:H, :], buf[0:H, :], start=first, stop=last)
        b = g.tensor.matmul(T.yb[:, 0:H], T.vt2[H:128, :], buf[H:128, :], start=first, stop=last)
        if last:
            a.then_inc(S.fa, 1)
            b.then_inc(S.fb, 1)

    g.vector.wait_ge(S.fa, 1)
    g.vector.tensor_tensor(T.ys[:, 0:H], T.xs[:, 0:H], T.ya[:, 0:H], AluOpType.subtract).then_inc(S.yv, 1)
    g.vector.wait_ge(S.fb, 1)
    g.vector.tensor_tensor(T.ys[:, H:128], T.xs[:, H:128], T.yb[:, 0:H], AluOpType.subtract).then_inc(S.yv, 1)
    g.sync.wait_ge(S.yv, 2)
    g.sync.dma_start(T.y[:], T.ys[:]).then_inc(S.st, 16)
    g.sync.wait_ge(S.st, 16)
    g.wait_ge(S.loc, sent)
